import numpy as np
import ml_dtypes


def mxq(x, axis, fmt="e4m3"):
    dtype, down = {"e4m3": (ml_dtypes.float8_e4m3fn, 7), "e5m2": (ml_dtypes.float8_e5m2, 14)}[fmt]
    v = np.moveaxis(np.asarray(x, np.float32).astype(ml_dtypes.bfloat16).astype(np.float64), axis, -1)
    blocks = v.reshape(v.shape[:-1] + (-1, 32))
    amax = np.abs(blocks).max(-1, keepdims=True)
    byte = np.maximum(np.where(amax > 0, np.frexp(amax)[1] - 1 + 127, 0) - down, 1)
    scale = np.exp2(byte - 127.0)
    codes = (blocks / scale).astype(np.float32).astype(dtype).astype(np.float64)
    return np.moveaxis((codes * scale).reshape(v.shape), -1, axis)


WIDE = False


def mx_kscale(k, group=512):
    if not WIDE:
        return np.ones(k)
    levels = np.array([10, -10, 5, -5, 0])
    if group != 512:
        return np.exp2(np.random.permutation(np.resize(levels, k // group))).repeat(group)
    if k % 512:
        return np.exp2(np.random.permutation(np.resize(levels, k // 32))).repeat(32)
    a = np.empty((k // 512, 16))
    for p in range(k // 512):
        a[p, :8] = np.random.permutation(np.resize(levels, 8))
        for g in range(8):
            far = levels[np.abs(levels - a[p, g]) >= 10]
            a[p, g + 8] = far[np.random.randint(len(far))]
    return np.exp2(a.ravel()).repeat(32)


def f64(x):
    return np.asarray(x).astype(np.float64)


def striped(idx):
    return np.tile(np.asarray(idx).reshape(-1, 16).T, (8, 1)).astype(np.uint16)


def unstriped(offs):
    return offs[:16].T.reshape(-1).astype(np.int64)


H, KV, D, NQ, N = 2, 2, 256, 512, 512


def setup_inputs():
    n = np.random.standard_normal
    s = mx_kscale(D, 0)[:, None]
    u = mx_kscale(N)
    t = np.random.uniform(0.5, 2.0, N) * u
    v = n((KV, N, 128))
    return {
        "qT": (n((H, D, NQ)) * s * (0.70 / np.sqrt(D))).astype(np.float32),
        "kT": (n((KV, D, N)) / s).astype(np.float32),
        "t": t.reshape(N, 1).astype(np.float32),
        "v": (v / t[:, None]).astype(np.float32),
        "mask": (np.arange(N)[:, None] <= np.sort(np.random.randint(N // 4, N, NQ))[None, :]).astype(np.float32),
    }


def reference(qT, kT, t, v, mask):
    a = mxq(f64(kT), 1, "e4m3").transpose(0, 2, 1) @ mxq(f64(qT), 1, "e4m3")
    p = 1.0 / (1.0 + np.exp(-a))
    p = p * f64(mask)
    w = p * f64(t)
    y = mxq(w, 1, "e4m3").transpose(0, 2, 1) @ mxq(f64(v), 1, "e4m3")
    y = y / 16.0
    return y

@@ -1,0 +1,285 @@
+from contextlib import ExitStack
+
+import concourse.mybir as mybir
+
+H, D, NQ, N, E = 2, 256, 512, 512, 128
+FLOPS = 2 * H * N * NQ * D + 2 * H * NQ * N * E
+
+F32 = mybir.dt.float32
+BF16 = mybir.dt.bfloat16
+U32 = mybir.dt.uint32
+U8 = mybir.dt.uint8
+FP8X4 = mybir.dt.float8_e4m3fn_x4
+ACT = mybir.ActivationFunctionType
+ALU = mybir.AluOpType
+
+P = 128
+PACK = 4
+ROWS = 64
+QC = 128
+CHUNKS = NQ // QC
+HALF = 64
+K_SPLIT = 44
+
+
+def tile_rows_sigmoid_mask_kernel(tc, qT, kT, t, v, mask, out):
+    nc = tc.nc
+    q_hbm = qT.rearrange("h (p j) q -> (h p) j q", j=PACK)
+    k_hbm = kT.rearrange("h (p j) i -> (h p) j i", j=PACK)
+    v_hbm = v.rearrange("h (p r) e -> p h (r e)", r=PACK)
+    t_hbm = t.rearrange("(p r) one -> p (r one)", r=PACK)
+    m_hbm = mask.rearrange("(p r) q -> p r q", r=PACK)
+    o_hbm = out.rearrange("h (c p) e -> c p h e", p=P)
+
+    with ExitStack() as ctx:
+        keep = ctx.enter_context(tc.tile_pool(name="keep", bufs=1))
+        psum = ctx.enter_context(tc.psum_pool(name="psum", bufs=1))
+        ctx.enter_context(tc.manual_schedule())
+
+        def sb(name, shape, dtype):
+            return keep.tile(shape, dtype, name=name, align_bytes=64)
+
+        t_sb = sb("t_sb", [P, PACK], F32)
+        warm_in = sb("warm_in", [P, 1], F32)
+        warm_out = sb("warm_out", [P, 1], F32)
+        k_raw = [sb("k_raw%d" % u, [P, PACK, N // 2], F32) for u in range(2)]
+        k_bf = sb("k_bf", [P, PACK, P, PACK], BF16)
+        k_codes = sb("k_codes", [P, PACK * P], U32)
+        k_scales = sb("k_scales", [P, PACK * P], U8)
+        v_raw = [sb("v_raw%d" % h, [P, PACK * E], F32) for h in range(H)]
+        v_bf = sb("v_bf", [P, H, E * PACK], BF16)
+        v_codes = sb("v_codes", [P, H * E], U32)
+        v_scales = sb("v_scales", [P, H * E], U8)
+        q_bf = [sb("q_bf%d" % c, [P, QC * PACK], BF16) for c in range(CHUNKS)]
+        q_codes = [sb("q_codes%d" % c, [P, QC], U32) for c in range(CHUNKS)]
+        q_scales = [sb("q_scales%d" % c, [P, QC], U8) for c in range(CHUNKS)]
+        tm = [sb("tm%d" % c, [P, PACK, QC], F32) for c in range(CHUNKS)]
+        sig = [[sb("sig%d_%d" % (c, h), [P, PACK, QC], F32) for h in range(H)] for c in range(CHUNKS)]
+        w_bf = [[sb("w_bf%d_%d" % (c, h), [P, QC * PACK], BF16) for h in range(H)] for c in range(CHUNKS)]
+        w_codes = [[sb("w_codes%d_%d" % (c, h), [P, QC], U32) for h in range(H)] for c in range(CHUNKS)]
+        w_scales = [[sb("w_scales%d_%d" % (c, h), [P, QC], U8) for h in range(H)] for c in range(CHUNKS)]
+        res = [[sb("res%d_%d" % (c, h), [P, E], F32) for h in range(H)] for c in range(CHUNKS)]
+        q_raw = {}
+        m_raw = {}
+        banks = {}
+        ybanks = {}
+
+        def load_cols(store, src, name, c0, c1):
+            raw = sb("%s%d" % (name, c0), [P, PACK, (c1 - c0) * QC], F32)
+            nc.sync.dma_start(out=raw[:], in_=src[:, :, c0 * QC : c1 * QC])
+            for c in range(c0, c1):
+                store[c] = raw[:, :, (c - c0) * QC : (c - c0 + 1) * QC]
+
+        def load_q(c0, c1):
+            load_cols(q_raw, q_hbm, "q_raw", c0, c1)
+
+        def load_m(c0, c1):
+            load_cols(m_raw, m_hbm, "m_raw", c0, c1)
+
+        def load_k(u):
+            nc.sync.dma_start(out=k_raw[u][:], in_=k_hbm[:, :, u * (N // 2) : (u + 1) * (N // 2)])
+
+        def load_vh(h):
+            nc.sync.dma_start(out=v_raw[h][:], in_=v_hbm[:, h, :])
+
+        def cast(eng, dst, src):
+            if eng == "V":
+                nc.vector.tensor_copy(out=dst, in_=src)
+            else:
+                nc.scalar.copy(out=dst, in_=src)
+
+        def group(eng, dst, src):
+            cast(
+                eng,
+                dst.rearrange("p (c i j) -> p c j i", i=4, j=PACK),
+                src.rearrange("p j (c i) -> p c j i", i=4),
+            )
+
+        def group_q(eng, c):
+            group(eng, q_bf[c][:], q_raw[c])
+
+        def group_v(eng, h):
+            group(eng, v_bf[:, h, :], v_raw[h][:].rearrange("p (r e) -> p r e", r=PACK))
+
+        def group_k(eng, u, s0, s1):
+            cast(
+                eng,
+                k_bf[:, :, u * HALF + s0 : u * HALF + s1, :].rearrange("p r s j -> p s r j"),
+                k_raw[u][:, :, PACK * s0 : PACK * s1].rearrange("p j (s r) -> p s r j", r=PACK),
+            )
+
+        def quant(codes, scales, src):
+            nc.vector.quantize_mx(out=codes.bitcast(FP8X4), scales=scales, in_=src)
+
+        def quant_k(u, r):
+            cols = slice(r * P + u * HALF, r * P + (u + 1) * HALF)
+            quant(
+                k_codes[:, cols],
+                k_scales[:, cols],
+                k_bf[:, r, u * HALF : (u + 1) * HALF, :].rearrange("p s j -> p (s j)"),
+            )
+
+        def quant_q(c):
+            quant(q_codes[c][:], q_scales[c][:], q_bf[c][:])
+
+        def quant_vh(h):
+            cols = slice(h * E, (h + 1) * E)
+            quant(v_codes[:, cols], v_scales[:, cols], v_bf[:, h, :])
+
+        def quant_w(c, h):
+            quant(w_codes[c][h][:], w_scales[c][h][:], w_bf[c][h][:])
+
+        def scores(c):
+            for h in range(H):
+                banks[c, h] = psum.tile([P, PACK, QC], F32, name="score%d" % h, tag="score%d" % h, bufs=3)
+            for r in range(PACK):
+                cols = slice(r * P, (r + 1) * P)
+                for h in range(H):
+                    rows = slice(h * ROWS, (h + 1) * ROWS)
+                    nc.tensor.matmul_mx(
+                        out=banks[c, h][:, r, :],
+                        lhsT=k_codes[rows, cols].bitcast(FP8X4),
+                        lhsT_scale=k_scales[rows, cols],
+                        rhs=q_codes[c][rows, :].bitcast(FP8X4),
+                        rhs_scale=q_scales[c][rows, :],
+                        start=True,
+                        stop=True,
+                    )
+
+        def sigmoid(c, h):
+            nc.scalar.activation(out=sig[c][h][:], in_=banks[c, h][:], func=ACT.Sigmoid)
+
+        def scale_mask(eng, c):
+            for r in range(PACK):
+                if eng == "V":
+                    nc.vector.tensor_scalar(
+                        out=tm[c][:, r, :], in0=m_raw[c][:, r, :], scalar1=t_sb[:, r : r + 1], scalar2=None, op0=ALU.mult
+                    )
+                else:
+                    nc.scalar.activation(out=tm[c][:, r, :], in_=m_raw[c][:, r, :], func=ACT.Copy, scale=t_sb[:, r : r + 1])
+
+        def weigh(c, h):
+            nc.vector.tensor_tensor(
+                out=w_bf[c][h][:].rearrange("p (c i r) -> p c r i", i=4, r=PACK),
+                in0=sig[c][h][:].rearrange("p r (c i) -> p c r i", i=4),
+                in1=tm[c][:].rearrange("p r (c i) -> p c r i", i=4),
+                op=ALU.mult,
+            )
+
+        def values(c, h):
+            ybanks[c, h] = psum.tile([P, E], F32, name="ybank", tag="ybank", bufs=2)
+            cols = slice(h * E, (h + 1) * E)
+            nc.tensor.matmul_mx(
+                out=ybanks[c, h][:],
+                lhsT=w_codes[c][h][:].bitcast(FP8X4),
+                lhsT_scale=w_scales[c][h][:],
+                rhs=v_codes[:, cols].bitcast(FP8X4),
+                rhs_scale=v_scales[:, cols],
+                start=True,
+                stop=True,
+            )
+
+        def finish_h(eng, c, h):
+            if eng == "V":
+                nc.vector.tensor_scalar(out=res[c][h][:], in0=ybanks[c, h][:], scalar1=1.0 / 16.0, scalar2=None, op0=ALU.mult)
+            else:
+                nc.scalar.activation(out=res[c][h][:], in_=ybanks[c, h][:], func=ACT.Copy, scale=1.0 / 16.0)
+
+        def store_h(c, h):
+            nc.sync.dma_start(out=o_hbm[c][:, h, :], in_=res[c][h][:])
+
+        nc.scalar.dma_start(out=t_sb[:], in_=t_hbm)
+        nc.vector.memset(warm_in[:], 0.0)
+        nc.scalar.activation(out=warm_out[:], in_=warm_in[:], func=ACT.Sigmoid)
+        load_k(0)
+        load_k(1)
+        load_q(0, 1)
+        load_q(1, 2)
+        load_m(0, 1)
+        load_q(2, 3)
+        load_vh(0)
+        load_m(1, 2)
+        load_q(3, 4)
+        load_vh(1)
+        load_m(2, 3)
+        load_m(3, 4)
+        group_k("V", 0, 0, 44)
+        group_k("S", 0, 44, 64)
+        quant_k(0, 0)
+        quant_k(0, 1)
+        quant_k(0, 2)
+        quant_k(0, 3)
+        group_k("V", 1, 0, 44)
+        group_k("S", 1, 44, 64)
+        group_q("V", 0)
+        quant_k(1, 0)
+        quant_q(0)
+        quant_k(1, 1)
+        quant_k(1, 2)
+        quant_k(1, 3)
+        scores(0)
+        group_q("S", 1)
+        quant_q(1)
+        scores(1)
+        scale_mask("V", 0)
+        group_q("V", 2)
+        group_v("V", 0)
+        quant_q(2)
+        quant_vh(0)
+        scores(2)
+        sigmoid(0, 0)
+        sigmoid(0, 1)
+        weigh(0, 0)
+        weigh(0, 1)
+        sigmoid(1, 0)
+        sigmoid(1, 1)
+        scale_mask("V", 1)
+        group_q("V", 3)
+        quant_w(0, 0)
+        quant_w(0, 1)
+        quant_q(3)
+        scores(3)
+        sigmoid(2, 0)
+        group_v("S", 1)
+        sigmoid(2, 1)
+        weigh(1, 0)
+        weigh(1, 1)
+        quant_vh(1)
+        values(0, 0)
+        values(0, 1)
+        quant_w(1, 0)
+        quant_w(1, 1)
+        scale_mask("S", 2)
+        scale_mask("S", 3)
+        weigh(2, 0)
+        weigh(2, 1)
+        sigmoid(3, 0)
+        finish_h("S", 0, 0)
+        finish_h("S", 0, 1)
+        store_h(0, 0)
+        store_h(0, 1)
+        values(1, 0)
+        values(1, 1)
+        sigmoid(3, 1)
+        quant_w(2, 0)
+        finish_h("S", 1, 0)
+        finish_h("S", 1, 1)
+        store_h(1, 0)
+        store_h(1, 1)
+        weigh(3, 0)
+        quant_w(2, 1)
+        values(2, 0)
+        values(2, 1)
+        weigh(3, 1)
+        finish_h("S", 2, 0)
+        finish_h("S", 2, 1)
+        store_h(2, 0)
+        store_h(2, 1)
+        quant_w(3, 0)
+        quant_w(3, 1)
+        values(3, 0)
+        values(3, 1)
+        finish_h("S", 3, 0)
+        finish_h("V", 3, 1)
+        store_h(3, 0)
+        store_h(3, 1)

@@ -76,7 +76,8 @@ def tile_rows_sigmoid_mask_kernel(tc, qT, kT, t, v, mask, out):
         def load_m(c0, c1):
             load_cols(m_raw, m_hbm, "m_raw", c0, c1)
 
-        def load_k(u):
+        def load_k(s0, s1):
+            u = s0 // HALF
             nc.sync.dma_start(out=k_raw[u][:], in_=k_hbm[:, :, u * (N // 2) : (u + 1) * (N // 2)])
 
         def load_vh(h):
@@ -91,17 +92,23 @@ def tile_rows_sigmoid_mask_kernel(tc, qT, kT, t, v, mask, out):
         def group(eng, dst, src):
             cast(
                 eng,
-                dst.rearrange("p (c i j) -> p c j i", i=4, j=PACK),
-                src.rearrange("p j (c i) -> p c j i", i=4),
+                dst.rearrange("p (c i j) -> p c j i", i=2, j=PACK),
+                src.rearrange("p j (c i) -> p c j i", i=2),
             )
 
         def group_q(eng, c):
             group(eng, q_bf[c][:], q_raw[c])
 
+        def split_q(c, n):
+            group("V", q_bf[c][:, : n * PACK], q_raw[c][:, :, :n])
+            group("S", q_bf[c][:, n * PACK :], q_raw[c][:, :, n:])
+
         def group_v(eng, h):
             group(eng, v_bf[:, h, :], v_raw[h][:].rearrange("p (r e) -> p r e", r=PACK))
 
-        def group_k(eng, u, s0, s1):
+        def group_k(eng, g0, g1):
+            u = g0 // HALF
+            s0, s1 = g0 - u * HALF, g1 - u * HALF
             cast(
                 eng,
                 k_bf[:, :, u * HALF + s0 : u * HALF + s1, :].rearrange("p r s j -> p s r j"),
@@ -129,25 +136,23 @@ def tile_rows_sigmoid_mask_kernel(tc, qT, kT, t, v, mask, out):
         def quant_w(c, h):
             quant(w_codes[c][h][:], w_scales[c][h][:], w_bf[c][h][:])
 
-        def scores(c):
-            for h in range(H):
-                banks[c, h] = psum.tile([P, PACK, QC], F32, name="score%d" % h, tag="score%d" % h, bufs=3)
-            for r in range(PACK):
+        def scores(c, h, r0, r1):
+            banks[c, h, r0] = psum.tile([P, PACK, QC], F32, name="score%d" % h, tag="score%d" % h, bufs=2)
+            rows = slice(h * ROWS, (h + 1) * ROWS)
+            for r in range(r0, r1):
                 cols = slice(r * P, (r + 1) * P)
-                for h in range(H):
-                    rows = slice(h * ROWS, (h + 1) * ROWS)
-                    nc.tensor.matmul_mx(
-                        out=banks[c, h][:, r, :],
-                        lhsT=k_codes[rows, cols].bitcast(FP8X4),
-                        lhsT_scale=k_scales[rows, cols],
-                        rhs=q_codes[c][rows, :].bitcast(FP8X4),
-                        rhs_scale=q_scales[c][rows, :],
-                        start=True,
-                        stop=True,
-                    )
+                nc.tensor.matmul_mx(
+                    out=banks[c, h, r0][:, r, :],
+                    lhsT=k_codes[rows, cols].bitcast(FP8X4),
+                    lhsT_scale=k_scales[rows, cols],
+                    rhs=q_codes[c][rows, :].bitcast(FP8X4),
+                    rhs_scale=q_scales[c][rows, :],
+                    start=True,
+                    stop=True,
+                )
 
-        def sigmoid(c, h):
-            nc.scalar.activation(out=sig[c][h][:], in_=banks[c, h][:], func=ACT.Sigmoid)
+        def sigmoid(c, h, r0, r1):
+            nc.scalar.activation(out=sig[c][h][:, r0:r1, :], in_=banks[c, h, r0][:, r0:r1, :], func=ACT.Sigmoid)
 
         def scale_mask(eng, c):
             for r in range(PACK):
@@ -160,14 +165,14 @@ def tile_rows_sigmoid_mask_kernel(tc, qT, kT, t, v, mask, out):
 
         def weigh(c, h):
             nc.vector.tensor_tensor(
-                out=w_bf[c][h][:].rearrange("p (c i r) -> p c r i", i=4, r=PACK),
-                in0=sig[c][h][:].rearrange("p r (c i) -> p c r i", i=4),
-                in1=tm[c][:].rearrange("p r (c i) -> p c r i", i=4),
+                out=w_bf[c][h][:].rearrange("p (c i r) -> p c r i", i=2, r=PACK),
+                in0=sig[c][h][:].rearrange("p r (c i) -> p c r i", i=2),
+                in1=tm[c][:].rearrange("p r (c i) -> p c r i", i=2),
                 op=ALU.mult,
             )
 
         def values(c, h):
-            ybanks[c, h] = psum.tile([P, E], F32, name="ybank", tag="ybank", bufs=2)
+            ybanks[c, h] = psum.tile([P, E], F32, name="ybank", tag="ybank", bufs=4)
             cols = slice(h * E, (h + 1) * E)
             nc.tensor.matmul_mx(
                 out=ybanks[c, h][:],
@@ -186,89 +191,96 @@ def tile_rows_sigmoid_mask_kernel(tc, qT, kT, t, v, mask, out):
                 nc.scalar.activation(out=res[c][h][:], in_=ybanks[c, h][:], func=ACT.Copy, scale=1.0 / 16.0)
 
         def store_h(c, h):
-            nc.sync.dma_start(out=o_hbm[c][:, h, :], in_=res[c][h][:])
+            queue = nc.scalar if (c, h) == (CHUNKS - 1, H - 1) else nc.sync
+            queue.dma_start(out=o_hbm[c][:, h, :], in_=res[c][h][:])
 
         nc.scalar.dma_start(out=t_sb[:], in_=t_hbm)
         nc.vector.memset(warm_in[:], 0.0)
         nc.scalar.activation(out=warm_out[:], in_=warm_in[:], func=ACT.Sigmoid)
-        load_k(0)
-        load_k(1)
+        load_k(0, 64)
+        load_k(64, 128)
         load_q(0, 1)
         load_q(1, 2)
         load_m(0, 1)
         load_q(2, 3)
-        load_vh(0)
         load_m(1, 2)
         load_q(3, 4)
-        load_vh(1)
         load_m(2, 3)
+        load_vh(0)
         load_m(3, 4)
-        group_k("V", 0, 0, 44)
-        group_k("S", 0, 44, 64)
+        load_vh(1)
+        group_k("V", 0, 44)
+        group_k("S", 44, 64)
         quant_k(0, 0)
         quant_k(0, 1)
         quant_k(0, 2)
         quant_k(0, 3)
-        group_k("V", 1, 0, 44)
-        group_k("S", 1, 44, 64)
-        group_q("V", 0)
+        group_k("V", 64, 108)
+        group_k("S", 108, 128)
+        split_q(0, 96)
         quant_k(1, 0)
         quant_q(0)
         quant_k(1, 1)
         quant_k(1, 2)
         quant_k(1, 3)
-        scores(0)
+        scores(0, 0, 0, 2)
+        scores(0, 0, 2, 4)
+        scores(0, 1, 0, 4)
         group_q("S", 1)
-        quant_q(1)
-        scores(1)
         scale_mask("V", 0)
+        quant_q(1)
         group_q("V", 2)
-        group_v("V", 0)
-        quant_q(2)
-        quant_vh(0)
-        scores(2)
-        sigmoid(0, 0)
-        sigmoid(0, 1)
+        sigmoid(0, 0, 0, 2)
+        scores(1, 0, 0, 4)
+        scores(1, 1, 0, 4)
+        sigmoid(0, 0, 2, 4)
+        sigmoid(0, 1, 0, 4)
         weigh(0, 0)
+        quant_q(2)
+        scores(2, 0, 0, 4)
+        scores(2, 1, 0, 4)
         weigh(0, 1)
-        sigmoid(1, 0)
-        sigmoid(1, 1)
-        scale_mask("V", 1)
-        group_q("V", 3)
+        scale_mask("S", 1)
         quant_w(0, 0)
+        group_q("V", 3)
         quant_w(0, 1)
-        quant_q(3)
-        scores(3)
-        sigmoid(2, 0)
-        group_v("S", 1)
-        sigmoid(2, 1)
+        sigmoid(1, 0, 0, 4)
+        sigmoid(1, 1, 0, 4)
         weigh(1, 0)
+        quant_q(3)
+        scores(3, 0, 0, 4)
+        scores(3, 1, 0, 4)
         weigh(1, 1)
-        quant_vh(1)
-        values(0, 0)
-        values(0, 1)
+        group_v("V", 0)
         quant_w(1, 0)
         quant_w(1, 1)
+        quant_vh(0)
+        values(0, 0)
+        values(1, 0)
         scale_mask("S", 2)
-        scale_mask("S", 3)
+        sigmoid(2, 0, 0, 4)
+        sigmoid(2, 1, 0, 4)
         weigh(2, 0)
         weigh(2, 1)
-        sigmoid(3, 0)
-        finish_h("S", 0, 0)
-        finish_h("S", 0, 1)
-        store_h(0, 0)
-        store_h(0, 1)
-        values(1, 0)
-        values(1, 1)
-        sigmoid(3, 1)
+        scale_mask("S", 3)
+        sigmoid(3, 0, 0, 4)
+        sigmoid(3, 1, 0, 4)
+        group_v("V", 1)
         quant_w(2, 0)
+        quant_vh(1)
+        values(0, 1)
+        values(1, 1)
+        finish_h("S", 0, 0)
         finish_h("S", 1, 0)
+        finish_h("S", 0, 1)
         finish_h("S", 1, 1)
+        store_h(0, 0)
         store_h(1, 0)
+        store_h(0, 1)
         store_h(1, 1)
+        values(2, 0)
         weigh(3, 0)
         quant_w(2, 1)
-        values(2, 0)
         values(2, 1)
         weigh(3, 1)
         finish_h("S", 2, 0)
@@ -279,7 +291,7 @@ def tile_rows_sigmoid_mask_kernel(tc, qT, kT, t, v, mask, out):
         quant_w(3, 1)
         values(3, 0)
         values(3, 1)
-        finish_h("S", 3, 0)
-        finish_h("V", 3, 1)
+        finish_h("V", 3, 0)
+        finish_h("S", 3, 1)
         store_h(3, 0)
         store_h(3, 1)

@@ -92,8 +92,8 @@ def tile_rows_sigmoid_mask_kernel(tc, qT, kT, t, v, mask, out):
         def group(eng, dst, src):
             cast(
                 eng,
-                dst.rearrange("p (c i j) -> p c j i", i=2, j=PACK),
-                src.rearrange("p j (c i) -> p c j i", i=2),
+                dst.rearrange("p (c i j) -> p c j i", i=4, j=PACK),
+                src.rearrange("p j (c i) -> p c j i", i=4),
             )
 
         def group_q(eng, c):
@@ -165,9 +165,9 @@ def tile_rows_sigmoid_mask_kernel(tc, qT, kT, t, v, mask, out):
 
         def weigh(c, h):
             nc.vector.tensor_tensor(
-                out=w_bf[c][h][:].rearrange("p (c i r) -> p c r i", i=2, r=PACK),
-                in0=sig[c][h][:].rearrange("p r (c i) -> p c r i", i=2),
-                in1=tm[c][:].rearrange("p r (c i) -> p c r i", i=2),
+                out=w_bf[c][h][:].rearrange("p (c i r) -> p c r i", i=4, r=PACK),
+                in0=sig[c][h][:].rearrange("p r (c i) -> p c r i", i=4),
+                in1=tm[c][:].rearrange("p r (c i) -> p c r i", i=4),
                 op=ALU.mult,
             )
 
@@ -191,8 +191,7 @@ def tile_rows_sigmoid_mask_kernel(tc, qT, kT, t, v, mask, out):
                 nc.scalar.activation(out=res[c][h][:], in_=ybanks[c, h][:], func=ACT.Copy, scale=1.0 / 16.0)
 
         def store_h(c, h):
-            queue = nc.scalar if (c, h) == (CHUNKS - 1, H - 1) else nc.sync
-            queue.dma_start(out=o_hbm[c][:, h, :], in_=res[c][h][:])
+            nc.sync.dma_start(out=o_hbm[c][:, h, :], in_=res[c][h][:])
 
         nc.scalar.dma_start(out=t_sb[:], in_=t_hbm)
         nc.vector.memset(warm_in[:], 0.0)

from contextlib import ExitStack

import concourse.mybir as mybir

H, D, NQ, N, E = 2, 256, 512, 512, 128
FLOPS = 2 * H * N * NQ * D + 2 * H * NQ * N * E

F32 = mybir.dt.float32
BF16 = mybir.dt.bfloat16
U32 = mybir.dt.uint32
U8 = mybir.dt.uint8
FP8X4 = mybir.dt.float8_e4m3fn_x4
ACT = mybir.ActivationFunctionType
ALU = mybir.AluOpType

P = 128
PACK = 4
ROWS = 64
QC = 128
CHUNKS = NQ // QC
HALF = 64
K_SPLIT = 44


def tile_rows_sigmoid_mask_kernel(tc, qT, kT, t, v, mask, out):
    nc = tc.nc
    q_hbm = qT.rearrange("h (p j) q -> (h p) j q", j=PACK)
    k_hbm = kT.rearrange("h (p j) i -> (h p) j i", j=PACK)
    v_hbm = v.rearrange("h (p r) e -> p h (r e)", r=PACK)
    t_hbm = t.rearrange("(p r) one -> p (r one)", r=PACK)
    m_hbm = mask.rearrange("(p r) q -> p r q", r=PACK)
    o_hbm = out.rearrange("h (c p) e -> c p h e", p=P)

    with ExitStack() as ctx:
        keep = ctx.enter_context(tc.tile_pool(name="keep", bufs=1))
        psum = ctx.enter_context(tc.psum_pool(name="psum", bufs=1))
        ctx.enter_context(tc.manual_schedule())

        def sb(name, shape, dtype):
            return keep.tile(shape, dtype, name=name, align_bytes=64)

        t_sb = sb("t_sb", [P, PACK], F32)
        warm_in = sb("warm_in", [P, 1], F32)
        warm_out = sb("warm_out", [P, 1], F32)
        k_raw = [sb("k_raw%d" % u, [P, PACK, N // 2], F32) for u in range(2)]
        k_bf = sb("k_bf", [P, PACK, P, PACK], BF16)
        k_codes = sb("k_codes", [P, PACK * P], U32)
        k_scales = sb("k_scales", [P, PACK * P], U8)
        v_raw = [sb("v_raw%d" % h, [P, PACK * E], F32) for h in range(H)]
        v_bf = sb("v_bf", [P, H, E * PACK], BF16)
        v_codes = sb("v_codes", [P, H * E], U32)
        v_scales = sb("v_scales", [P, H * E], U8)
        q_bf = [sb("q_bf%d" % c, [P, QC * PACK], BF16) for c in range(CHUNKS)]
        q_codes = [sb("q_codes%d" % c, [P, QC], U32) for c in range(CHUNKS)]
        q_scales = [sb("q_scales%d" % c, [P, QC], U8) for c in range(CHUNKS)]
        tm = [sb("tm%d" % c, [P, PACK, QC], F32) for c in range(CHUNKS)]
        sig = [[sb("sig%d_%d" % (c, h), [P, PACK, QC], F32) for h in range(H)] for c in range(CHUNKS)]
        w_bf = [[sb("w_bf%d_%d" % (c, h), [P, QC * PACK], BF16) for h in range(H)] for c in range(CHUNKS)]
        w_codes = [[sb("w_codes%d_%d" % (c, h), [P, QC], U32) for h in range(H)] for c in range(CHUNKS)]
        w_scales = [[sb("w_scales%d_%d" % (c, h), [P, QC], U8) for h in range(H)] for c in range(CHUNKS)]
        res = [[sb("res%d_%d" % (c, h), [P, E], F32) for h in range(H)] for c in range(CHUNKS)]
        q_raw = {}
        m_raw = {}
        banks = {}
        ybanks = {}

        def load_cols(store, src, name, c0, c1):
            raw = sb("%s%d" % (name, c0), [P, PACK, (c1 - c0) * QC], F32)
            nc.sync.dma_start(out=raw[:], in_=src[:, :, c0 * QC : c1 * QC])
            for c in range(c0, c1):
                store[c] = raw[:, :, (c - c0) * QC : (c - c0 + 1) * QC]

        def load_q(c0, c1):
            load_cols(q_raw, q_hbm, "q_raw", c0, c1)

        def load_m(c0, c1):
            load_cols(m_raw, m_hbm, "m_raw", c0, c1)

        def load_k(s0, s1):
            u = s0 // HALF
            nc.sync.dma_start(out=k_raw[u][:], in_=k_hbm[:, :, u * (N // 2) : (u + 1) * (N // 2)])

        def load_vh(h):
            nc.sync.dma_start(out=v_raw[h][:], in_=v_hbm[:, h, :])

        def cast(eng, dst, src):
            if eng == "V":
                nc.vector.tensor_copy(out=dst, in_=src)
            else:
                nc.scalar.copy(out=dst, in_=src)

        def group(eng, dst, src):
            cast(
                eng,
                dst.rearrange("p (c i j) -> p c j i", i=4, j=PACK),
                src.rearrange("p j (c i) -> p c j i", i=4),
            )

        def group_q(eng, c):
            group(eng, q_bf[c][:], q_raw[c])

        def split_q(c, n):
            group("V", q_bf[c][:, : n * PACK], q_raw[c][:, :, :n])
            group("S", q_bf[c][:, n * PACK :], q_raw[c][:, :, n:])

        def group_v(eng, h):
            group(eng, v_bf[:, h, :], v_raw[h][:].rearrange("p (r e) -> p r e", r=PACK))

        def group_k(eng, g0, g1):
            u = g0 // HALF
            s0, s1 = g0 - u * HALF, g1 - u * HALF
            cast(
                eng,
                k_bf[:, :, u * HALF + s0 : u * HALF + s1, :].rearrange("p r s j -> p s r j"),
                k_raw[u][:, :, PACK * s0 : PACK * s1].rearrange("p j (s r) -> p s r j", r=PACK),
            )

        def quant(codes, scales, src):
            nc.vector.quantize_mx(out=codes.bitcast(FP8X4), scales=scales, in_=src)

        def quant_k(u, r):
            cols = slice(r * P + u * HALF, r * P + (u + 1) * HALF)
            quant(
                k_codes[:, cols],
                k_scales[:, cols],
                k_bf[:, r, u * HALF : (u + 1) * HALF, :].rearrange("p s j -> p (s j)"),
            )

        def quant_q(c):
            quant(q_codes[c][:], q_scales[c][:], q_bf[c][:])

        def quant_vh(h):
            cols = slice(h * E, (h + 1) * E)
            quant(v_codes[:, cols], v_scales[:, cols], v_bf[:, h, :])

        def quant_w(c, h):
            quant(w_codes[c][h][:], w_scales[c][h][:], w_bf[c][h][:])

        def scores(c, h, r0, r1):
            banks[c, h, r0] = psum.tile([P, PACK, QC], F32, name="score%d" % h, tag="score%d" % h, bufs=2)
            rows = slice(h * ROWS, (h + 1) * ROWS)
            for r in range(r0, r1):
                cols = slice(r * P, (r + 1) * P)
                nc.tensor.matmul_mx(
                    out=banks[c, h, r0][:, r, :],
                    lhsT=k_codes[rows, cols].bitcast(FP8X4),
                    lhsT_scale=k_scales[rows, cols],
                    rhs=q_codes[c][rows, :].bitcast(FP8X4),
                    rhs_scale=q_scales[c][rows, :],
                    start=True,
                    stop=True,
                )

        def sigmoid(c, h, r0, r1):
            nc.scalar.activation(out=sig[c][h][:, r0:r1, :], in_=banks[c, h, r0][:, r0:r1, :], func=ACT.Sigmoid)

        def scale_mask(eng, c):
            for r in range(PACK):
                if eng == "V":
                    nc.vector.tensor_scalar(
                        out=tm[c][:, r, :], in0=m_raw[c][:, r, :], scalar1=t_sb[:, r : r + 1], scalar2=None, op0=ALU.mult
                    )
                else:
                    nc.scalar.activation(out=tm[c][:, r, :], in_=m_raw[c][:, r, :], func=ACT.Copy, scale=t_sb[:, r : r + 1])

        def weigh(c, h):
            nc.vector.tensor_tensor(
                out=w_bf[c][h][:].rearrange("p (c i r) -> p c r i", i=4, r=PACK),
                in0=sig[c][h][:].rearrange("p r (c i) -> p c r i", i=4),
                in1=tm[c][:].rearrange("p r (c i) -> p c r i", i=4),
                op=ALU.mult,
            )

        def values(c, h):
            ybanks[c, h] = psum.tile([P, E], F32, name="ybank", tag="ybank", bufs=4)
            cols = slice(h * E, (h + 1) * E)
            nc.tensor.matmul_mx(
                out=ybanks[c, h][:],
                lhsT=w_codes[c][h][:].bitcast(FP8X4),
                lhsT_scale=w_scales[c][h][:],
                rhs=v_codes[:, cols].bitcast(FP8X4),
                rhs_scale=v_scales[:, cols],
                start=True,
                stop=True,
            )

        def finish_h(eng, c, h):
            if eng == "V":
                nc.vector.tensor_scalar(out=res[c][h][:], in0=ybanks[c, h][:], scalar1=1.0 / 16.0, scalar2=None, op0=ALU.mult)
            else:
                nc.scalar.activation(out=res[c][h][:], in_=ybanks[c, h][:], func=ACT.Copy, scale=1.0 / 16.0)

        def store_h(c, h):
            nc.sync.dma_start(out=o_hbm[c][:, h, :], in_=res[c][h][:])

        nc.scalar.dma_start(out=t_sb[:], in_=t_hbm)
        nc.vector.memset(warm_in[:], 0.0)
        nc.scalar.activation(out=warm_out[:], in_=warm_in[:], func=ACT.Sigmoid)
        load_k(0, 64)
        load_k(64, 128)
        load_q(0, 1)
        load_q(1, 2)
        load_m(0, 1)
        load_q(2, 3)
        load_m(1, 2)
        load_q(3, 4)
        load_m(2, 3)
        load_vh(0)
        load_m(3, 4)
        load_vh(1)
        group_k("V", 0, 44)
        group_k("S", 44, 64)
        quant_k(0, 0)
        quant_k(0, 1)
        quant_k(0, 2)
        quant_k(0, 3)
        group_k("V", 64, 108)
        group_k("S", 108, 128)
        split_q(0, 96)
        quant_k(1, 0)
        quant_q(0)
        quant_k(1, 1)
        quant_k(1, 2)
        quant_k(1, 3)
        scores(0, 0, 0, 2)
        scores(0, 0, 2, 4)
        scores(0, 1, 0, 4)
        group_q("S", 1)
        scale_mask("V", 0)
        quant_q(1)
        group_q("V", 2)
        sigmoid(0, 0, 0, 2)
        scores(1, 0, 0, 4)
        scores(1, 1, 0, 4)
        sigmoid(0, 0, 2, 4)
        sigmoid(0, 1, 0, 4)
        weigh(0, 0)
        quant_q(2)
        scores(2, 0, 0, 4)
        scores(2, 1, 0, 4)
        weigh(0, 1)
        scale_mask("S", 1)
        quant_w(0, 0)
        group_q("V", 3)
        quant_w(0, 1)
        sigmoid(1, 0, 0, 4)
        sigmoid(1, 1, 0, 4)
        weigh(1, 0)
        quant_q(3)
        scores(3, 0, 0, 4)
        scores(3, 1, 0, 4)
        weigh(1, 1)
        group_v("V", 0)
        quant_w(1, 0)
        quant_w(1, 1)
        quant_vh(0)
        values(0, 0)
        values(1, 0)
        scale_mask("S", 2)
        sigmoid(2, 0, 0, 4)
        sigmoid(2, 1, 0, 4)
        weigh(2, 0)
        weigh(2, 1)
        scale_mask("S", 3)
        sigmoid(3, 0, 0, 4)
        sigmoid(3, 1, 0, 4)
        group_v("V", 1)
        quant_w(2, 0)
        quant_vh(1)
        values(0, 1)
        values(1, 1)
        finish_h("S", 0, 0)
        finish_h("S", 1, 0)
        finish_h("S", 0, 1)
        finish_h("S", 1, 1)
        store_h(0, 0)
        store_h(1, 0)
        store_h(0, 1)
        store_h(1, 1)
        values(2, 0)
        weigh(3, 0)
        quant_w(2, 1)
        values(2, 1)
        weigh(3, 1)
        finish_h("S", 2, 0)
        finish_h("S", 2, 1)
        store_h(2, 0)
        store_h(2, 1)
        quant_w(3, 0)
        quant_w(3, 1)
        values(3, 0)
        values(3, 1)
        finish_h("V", 3, 0)
        finish_h("S", 3, 1)
        store_h(3, 0)
        store_h(3, 1)
